import numpy as np
import ml_dtypes


def mxq(x, axis, fmt="e4m3"):
    dtype, down = {"e4m3": (ml_dtypes.float8_e4m3fn, 7), "e5m2": (ml_dtypes.float8_e5m2, 14)}[fmt]
    v = np.moveaxis(np.asarray(x, np.float32).astype(ml_dtypes.bfloat16).astype(np.float64), axis, -1)
    blocks = v.reshape(v.shape[:-1] + (-1, 32))
    amax = np.abs(blocks).max(-1, keepdims=True)
    byte = np.maximum(np.where(amax > 0, np.frexp(amax)[1] - 1 + 127, 0) - down, 1)
    scale = np.exp2(byte - 127.0)
    codes = (blocks / scale).astype(np.float32).astype(dtype).astype(np.float64)
    return np.moveaxis((codes * scale).reshape(v.shape), -1, axis)


WIDE = False


def mx_kscale(k):
    if not WIDE:
        return np.ones(k)
    levels = np.array([10, -10, 5, -5, 0])
    if k % 512:
        return np.exp2(np.random.permutation(np.resize(levels, k // 32))).repeat(32)
    a = np.empty((k // 512, 16))
    for p in range(k // 512):
        a[p, :8] = np.random.permutation(np.resize(levels, 8))
        for g in range(8):
            far = levels[np.abs(levels - a[p, g]) >= 10]
            a[p, g + 8] = far[np.random.randint(len(far))]
    return np.exp2(a.ravel()).repeat(32)


def f64(x):
    return np.asarray(x).astype(np.float64)


def striped(idx):
    return np.tile(np.asarray(idx).reshape(-1, 16).T, (8, 1)).astype(np.uint16)


def unstriped(offs):
    return offs[:16].T.reshape(-1).astype(np.int64)


E2M1 = np.array([0.0, 0.5, 1.0, 1.5, 2.0, 3.0, 4.0, 6.0, -0.0, -0.5, -1.0, -1.5, -2.0, -3.0, -4.0, -6.0])


def pack_weight(w, fmt):
    k, n = w.shape
    w = f64(np.asarray(w, np.float32).astype(ml_dtypes.bfloat16)).reshape(k // 32, 32, n)
    amax = np.abs(w).max(1)
    if fmt == "e4m3":
        byte = np.frexp(amax)[1] - 1 + 127 - 7
    else:
        mant, ex = np.frexp(amax / 6.0)
        byte = np.where(mant > 0.5, ex, ex - 1) + 127
    byte = np.clip(np.where(amax > 0, byte, 1), 1, 254)
    scaled = (w * np.exp2(127.0 - byte)[:, None, :]).reshape(k, n).astype(np.float32)
    by_word = np.ascontiguousarray(scaled.reshape(k // 512, 128, 4, n).transpose(0, 1, 3, 2))
    if fmt == "e4m3":
        words = by_word.astype(ml_dtypes.float8_e4m3fn).view(np.uint8)
    else:
        c = by_word.astype(ml_dtypes.float4_e2m1fn).view(np.uint8) & 0xF
        words = (c[..., 0::2] | (c[..., 1::2] << 4)).reshape(k // 512, 128, 2 * n)
    return np.ascontiguousarray(words), np.ascontiguousarray(byte.astype(np.uint8).reshape(k // 512, 16, n))


def unpack_weight(words, scales, fmt):
    g, _, n = scales.shape
    words = np.ascontiguousarray(words).reshape(g, 128, n, -1)
    if fmt == "e4m3":
        vals = words.view(ml_dtypes.float8_e4m3fn).astype(np.float64)
    else:
        nib = np.empty((g, 128, n, 4), np.uint8)
        nib[..., 0::2] = words & 0xF
        nib[..., 1::2] = words >> 4
        vals = E2M1[nib]
    vals = vals * np.repeat(np.exp2(scales.astype(np.float64) - 127.0), 8, axis=1)[..., None]
    return vals.transpose(0, 1, 3, 2).reshape(g * 512, n)


D, E, T, I, Q = 512, 512, 2048, 512, 128


def setup_inputs():
    n = np.random.standard_normal
    idx = np.random.permutation(T)[:I]
    fd = mx_kscale(D)
    fe = mx_kscale(E)
    keysp = pack_weight(n((D, T)) / fd[:, None], "e4m3")
    valsp = pack_weight(n((E, T)) / fe[:, None], "e4m3")
    return {
        "query": (n((D, Q)) * 0.6 / np.sqrt(D) * fd[:, None]).astype(np.float32),
        "keys_words": keysp[0],
        "keys_scales": keysp[1],
        "age": np.tile(np.random.uniform(0.0, 2.0, T), (128, 1)).astype(np.float32),
        "rate": (np.random.uniform(0.3, 1.2, (Q, 1))).astype(np.float32),
        "reserve": (np.random.uniform(20.0, 100.0, (Q, 1))).astype(np.float32),
        "gout": (n((E, Q)) * 1 / np.sqrt(E) * fe[:, None]).astype(np.float32),
        "vals_words": valsp[0],
        "vals_scales": valsp[1],
        "size": (np.random.uniform(0.5, 2.0, (1, I))).astype(np.float32),
        "dquery": (n((D, Q)) * 1.0 / np.sqrt(D) * fd[:, None]).astype(np.float32),
        "base": (0.5 * n((Q, T))).astype(np.float32),
        "offs": striped(idx),
    }


def reference(query, keys_words, keys_scales, age, rate, reserve, gout, vals_words, vals_scales, size, dquery, base, offs):
    idx = unstriped(offs)
    keysu = unpack_weight(keys_words, keys_scales, "e4m3")
    valsu = unpack_weight(vals_words, vals_scales, "e4m3")
    queryq = mxq(f64(query), 0, "e4m3")
    keysidxg = keysu[:, idx]
    a = queryq.T @ keysidxg
    dqueryq = mxq(f64(dquery), 0, "e4m3")
    ta = dqueryq.T @ keysidxg
    p = np.exp(a - f64(age)[:1][:, idx] * f64(rate))
    z = np.sum(p, axis=1, keepdims=True) + f64(reserve)
    goutq = mxq(f64(gout), 0, "e4m3")
    valsidxg = valsu[:, idx]
    c0 = goutq.T @ valsidxg
    dz = np.sum(c0 * p * f64(size) / np.square(z) * (-1.0), axis=1, keepdims=True)
    dp = c0 / z * f64(size) + dz
    tp = ta * p
    tz = np.sum(tp, axis=1, keepdims=True)
    tdz = np.sum((tp * f64(size) * c0 - tz * z * 2.0 * c0 * p * f64(size) / np.square(z)) / np.square(z) * (-1.0), axis=1, keepdims=True)
    tdp = tz * c0 / np.square(z) * (-1.0) * f64(size) + tdz
    tda = tdp * p + tp * dp
    gs = tda * 512.0
    gf = np.zeros((Q, T))
    gf[:, idx] = gs
    y = f64(base) + gf
    return y

@@ -1,0 +1,202 @@
+from contextlib import ExitStack
+
+import concourse.mybir as mybir
+from concourse.masks import make_identity
+
+D, E, T, I, Q = 512, 512, 2048, 512, 128
+FLOPS = 2 * Q * I * (2 * D + E)
+
+F32 = mybir.dt.float32
+BF16 = mybir.dt.bfloat16
+I32 = mybir.dt.int32
+U32 = mybir.dt.uint32
+U16 = mybir.dt.uint16
+U8 = mybir.dt.uint8
+FP8X4 = mybir.dt.float8_e4m3fn_x4
+ALU = mybir.AluOpType
+ACT = mybir.ActivationFunctionType
+
+P = 128
+PACK = 4
+SLOT_TILES = I // P
+OUT_CHUNKS = 4
+
+
+def tile_attend_hvfadereserve_s_kernel(tc, query, keys_words, keys_scales, age, rate, reserve, gout,
+                                        vals_words, vals_scales, size, dquery, base, offs, out):
+    nc = tc.nc
+    with ExitStack() as ctx:
+        sb = ctx.enter_context(tc.tile_pool(name="sb", bufs=1))
+        ps = ctx.enter_context(tc.psum_pool(name="ps", bufs=1))
+
+        def sbuf(name, shape, dtype, tag=None):
+            return sb.tile(shape, dtype, name=name, tag=tag or name, align_bytes=64)
+
+        offsets = sbuf("offsets", [P, I // 16], U16)
+        nc.sync.dma_start(offsets[:], offs)
+
+        key_bytes = sbuf("key_bytes", [P, T], U8)
+        age_row = sbuf("age_row", [P, T], F32)
+        val_bytes = sbuf("val_bytes", [P, T], U8)
+        nc.vector.memset(key_bytes[:].bitcast(I32), 0)
+        nc.vector.memset(age_row[:], 0.0)
+        nc.vector.memset(val_bytes[:].bitcast(I32), 0)
+
+        ident = sbuf("ident", [P, P], F32)
+        make_identity(nc, ident[:])
+
+        def load_scale_rows(queue, tile, scales):
+            for quad in range(4):
+                queue.dma_start(tile[32 * quad : 32 * quad + 4, :].bitcast(I32),
+                                scales[0, 4 * quad : 4 * quad + 4, :].bitcast(I32))
+
+        def load_words(name, words):
+            tile = sbuf(name, [P, T], I32)
+            nc.sync.dma_start(tile[:], words[0].rearrange("p n t -> p (n t)").bitcast(I32))
+            return tile
+
+        def load_rows(name, rows):
+            tile = sbuf(name, [P, PACK, Q], F32)
+            nc.sync.dma_start(tile[:], rows.rearrange("(p j) w -> p j w", j=PACK))
+            return tile
+
+        rate_col = sbuf("rate_col", [P, 1], F32)
+        nc.sync.dma_start(rate_col[:], rate)
+        key_words = load_words("key_words", keys_words)
+        load_scale_rows(nc.scalar, key_bytes, keys_scales)
+        nc.scalar.dma_start(age_row[0:1, :], age[0:1, :])
+        query_raw = load_rows("query_raw", query)
+        val_words = load_words("val_words", vals_words)
+        dquery_raw = load_rows("dquery_raw", dquery)
+        load_scale_rows(nc.sync, val_bytes, vals_scales)
+        gout_raw = load_rows("gout_raw", gout)
+        size_cols = sbuf("size_cols", [P, SLOT_TILES], F32)
+        nc.sync.dma_start(size_cols[:], size.rearrange("o (p c) -> p (o c)", p=P))
+        reserve_col = sbuf("reserve_col", [P, 1], F32)
+        nc.sync.dma_start(reserve_col[:], reserve)
+        base_sb = sbuf("base_sb", [P, T], F32)
+        nc.sync.dma_start(base_sb[:], base)
+
+        warm = sbuf("warm", [P, 1], F32)
+        nc.scalar.activation(warm[:], ident[:, 0:1], ACT.Exp)
+
+        def gather(name, window, dtype, tag=None):
+            tile = sbuf(name, [P, I], dtype, tag)
+            nc.vector.tensor_copy(tile[:], window.indirect(offsets[:]))
+            return tile
+
+        def interleave(name, raw):
+            tile = sbuf(name, [P, Q, PACK], BF16)
+            nc.scalar.copy(tile[:], raw[:].rearrange("p j w -> p w j"))
+            return tile
+
+        def quantize(name, grouped, tag):
+            codes = sbuf(name + "_codes", [P, Q], U32, tag)
+            scales = sbuf(name + "_scales", [P, Q], U8)
+            nc.vector.quantize_mx(codes[:].bitcast(FP8X4), scales[:], grouped[:].rearrange("p w j -> p (w j)"))
+            return codes, scales
+
+        def slot_major_product(name, words, scales, rows):
+            bank = ps.tile([P, SLOT_TILES, Q], F32, name=name)
+            for c in range(SLOT_TILES):
+                cols = slice(c * P, (c + 1) * P)
+                nc.tensor.matmul_mx(bank[:, c, :], lhsT=words[:, cols].bitcast(FP8X4), lhsT_scale=scales[:, cols],
+                                    rhs=rows[0][:].bitcast(FP8X4), rhs_scale=rows[1][:], start=True, stop=True)
+            return bank
+
+        key_scale_slots = gather("key_scale_slots", key_bytes[:], U8)
+        age_slots = gather("age_slots", age_row[:], F32)
+        placed = sbuf("placed", [P, T], F32, tag="key_bytes")
+        nc.gpsimd.memset(placed[:], 0.0)
+        key_slots = gather("key_slots", key_words[:].bitcast(U32), U32, tag="age_row")
+        query_mx = quantize("query", interleave("query_bf", query_raw), "key_words")
+
+        rate_rows = ps.tile([P, Q], F32, name="rate_rows")
+        nc.tensor.transpose(rate_rows[:], rate_col[:].to_broadcast([P, P]), ident[:])
+        age_turned = ps.tile([P, SLOT_TILES, P], F32, name="age_turned")
+        for c in range(SLOT_TILES):
+            nc.tensor.transpose(age_turned[:, c, :], age_slots[:, c * P : (c + 1) * P], ident[:])
+        neg_age = sbuf("neg_age", [P, SLOT_TILES], F32)
+        nc.scalar.activation(neg_age[:], age_turned[:, :, 0], ACT.Copy, scale=-1.0)
+        fade_t = sbuf("fade_t", [P, SLOT_TILES, Q], F32)
+        for c in range(SLOT_TILES):
+            nc.scalar.activation(fade_t[:, c, :], rate_rows[:], ACT.Copy, scale=neg_age[:, c : c + 1])
+        x = ps.tile([P, I], F32, name="x")
+        for c in range(SLOT_TILES):
+            nc.tensor.matmul(x[:, c * P : (c + 1) * P], lhsT=fade_t[:, c, :], rhs=ident[:], is_transpose=True,
+                             start=(c == 0), stop=False)
+
+        a_t = slot_major_product("a_t", key_slots, key_scale_slots, query_mx)
+        a_t_sb = sbuf("a_t_sb", [P, SLOT_TILES, Q], F32)
+        nc.scalar.copy(a_t_sb[:], a_t[:])
+        for c in range(SLOT_TILES):
+            nc.tensor.matmul(x[:, c * P : (c + 1) * P], lhsT=a_t_sb[:, c, :], rhs=ident[:], is_transpose=True,
+                             start=False, stop=(c == SLOT_TILES - 1))
+
+        size_rows = ps.tile([P, SLOT_TILES, P], F32, name="size_rows")
+        for c in range(SLOT_TILES):
+            nc.tensor.transpose(size_rows[:, c, :], size_cols[:, c : c + 1].to_broadcast([P, P]), ident[:])
+        weight_rows = sbuf("weight_rows", [P, I], F32)
+        nc.scalar.activation(weight_rows[:].rearrange("p (n c) -> p n c", c=SLOT_TILES),
+                             size_rows[:].rearrange("p c n -> p n c"), ACT.Copy, scale=-512.0)
+
+        val_scale_slots = gather("val_scale_slots", val_bytes[:], U8, tag="query_bf")
+        val_slots = gather("val_slots", val_words[:].bitcast(U32), U32, tag="val_bytes")
+        gout_mx = quantize("gout", interleave("gout_bf", gout_raw), "val_words")
+        dquery_mx = quantize("dquery", interleave("dquery_bf", dquery_raw), "gout_bf")
+
+        neg_x = sbuf("neg_x", [P, I], F32)
+        neg_max = sbuf("neg_max", [P, 1], F32)
+        nc.vector.tensor_scalar(neg_x[:], x[:], -1.0, 0.0, ALU.mult, ALU.min, accum_out=neg_max[:])
+        sink = sbuf("sink", [P, 1], F32)
+        nc.scalar.activation(sink[:], neg_max[:], ACT.Exp)
+        p = sbuf("p", [P, I], F32)
+        p_sum = sbuf("p_sum", [P, 1], F32)
+        nc.scalar.activation(p[:], neg_x[:], ACT.Exp, bias=neg_max[:], scale=-1.0, accum_out=p_sum[:])
+        z = sbuf("z", [P, 1], F32)
+        nc.scalar.activation(z[:], sink[:], ACT.Identity, bias=p_sum[:], scale=reserve_col[:])
+
+        def row_major_product(name, rows, words, scales):
+            bank = ps.tile([P, I], F32, name=name)
+            nc.tensor.matmul_mx(bank[:], lhsT=rows[0][:].bitcast(FP8X4), lhsT_scale=rows[1][:],
+                                rhs=words[:].bitcast(FP8X4), rhs_scale=scales[:], start=True, stop=True)
+            return bank
+
+        c0 = row_major_product("c0", gout_mx, val_slots, val_scale_slots)
+        ta = row_major_product("ta", dquery_mx, key_slots, key_scale_slots)
+        u = sbuf("u", [P, I], F32)
+        nc.vector.tensor_tensor(u[:], c0[:], weight_rows[:], ALU.mult)
+
+        up = sbuf("up", [P, I], F32)
+        up_sum = sbuf("up_sum", [P, 1], F32)
+        nc.vector.scalar_tensor_tensor(up[:], p[:], 1.0, u[:], ALU.mult, ALU.mult, accum_out=up_sum[:])
+        inv_z = sbuf("inv_z", [P, 1], F32)
+        nc.vector.reciprocal(inv_z[:], z[:])
+        tw = sbuf("tw", [P, I], F32)
+        mean_ta = sbuf("mean_ta", [P, 1], F32)
+        nc.vector.scalar_tensor_tensor(tw[:], p[:], inv_z[:], ta[:], ALU.mult, ALU.mult, accum_out=mean_ta[:])
+        mean_u = sbuf("mean_u", [P, 1], F32)
+        nc.scalar.activation(mean_u[:], up_sum[:], ACT.Copy, scale=inv_z[:])
+        w = sbuf("w", [P, I], F32)
+        nc.scalar.activation(w[:], p[:], ACT.Copy, scale=inv_z[:])
+        neg_mean_ta = sbuf("neg_mean_ta", [P, 1], F32)
+        nc.scalar.activation(neg_mean_ta[:], mean_ta[:], ACT.Copy, scale=-1.0)
+        up_factor = sbuf("up_factor", [P, 1], F32)
+        nc.scalar.activation(up_factor[:], mean_ta[:], ACT.Copy, scale=inv_z[:])
+        cross = sbuf("cross", [P, I], F32)
+        cross_sum = sbuf("cross_sum", [P, 1], F32)
+        nc.vector.scalar_tensor_tensor(cross[:], u[:], mean_u[:], tw[:], ALU.subtract, ALU.mult, accum_out=cross_sum[:])
+        part = sbuf("part", [P, I], F32)
+        nc.vector.scalar_tensor_tensor(part[:], up[:], up_factor[:], cross[:], ALU.mult, ALU.subtract)
+        shift = sbuf("shift", [P, 1], F32)
+        nc.scalar.activation(shift[:], mean_u[:], ACT.Identity, bias=cross_sum[:], scale=neg_mean_ta[:])
+        shift_w = sbuf("shift_w", [P, I], F32)
+        nc.scalar.activation(shift_w[:], w[:], ACT.Copy, scale=shift[:])
+        nc.vector.tensor_tensor(placed[:].indirect(offsets[:]), part[:], shift_w[:], ALU.add)
+
+        width = T // OUT_CHUNKS
+        for n in range(OUT_CHUNKS):
+            cols = slice(n * width, (n + 1) * width)
+            result = sbuf("result%d" % n, [P, width], F32)
+            nc.vector.tensor_tensor(result[:], placed[:, cols], base_sb[:, cols], ALU.add)
+            (nc.sync, nc.scalar)[n % 2].dma_start(out[:, cols], result[:])

@@ -36,57 +36,64 @@ def tile_attend_hvfadereserve_s_kernel(tc, query, keys_words, keys_scales, age, 
         nc.sync.dma_start(offsets[:], offs)
 
         key_bytes = sbuf("key_bytes", [P, T], U8)
-        age_row = sbuf("age_row", [P, T], F32)
         val_bytes = sbuf("val_bytes", [P, T], U8)
-        nc.vector.memset(key_bytes[:].bitcast(I32), 0)
-        nc.vector.memset(age_row[:], 0.0)
-        nc.vector.memset(val_bytes[:].bitcast(I32), 0)
-
+        age_row = sbuf("age_row", [P, T], F32)
+        warm = sbuf("warm", [P, 1], F32)
+        key_zero = key_bytes[:].bitcast(I32)
+        nc.vector.memset(key_zero[:, : T // 8], 0)
+        nc.gpsimd.memset(key_zero[:, T // 8 :], 0)
+        nc.gpsimd.memset(val_bytes[:].bitcast(I32), 0)
+        nc.gpsimd.memset(warm[:], 0.0)
+        nc.vector.memset(age_row[64:128, : T - 1], 0.0)
+        nc.vector.memset(age_row[64:128, T - 1 :], 0.0)
         ident = sbuf("ident", [P, P], F32)
         make_identity(nc, ident[:])
+        nc.gpsimd.memset(age_row[32:64, :], 0.0)
+        placed = sbuf("placed", [P, T], F32)
+        nc.gpsimd.memset(placed[:], 0.0)
 
         def load_scale_rows(queue, tile, scales):
             for quad in range(4):
                 queue.dma_start(tile[32 * quad : 32 * quad + 4, :].bitcast(I32),
                                 scales[0, 4 * quad : 4 * quad + 4, :].bitcast(I32))
 
-        def load_words(name, words):
-            tile = sbuf(name, [P, T], I32)
+        def load_words(name, words, tag=None):
+            tile = sbuf(name, [P, T], I32, tag)
             nc.sync.dma_start(tile[:], words[0].rearrange("p n t -> p (n t)").bitcast(I32))
             return tile
 
-        def load_rows(name, rows):
-            tile = sbuf(name, [P, PACK, Q], F32)
+        def load_rows(name, rows, tag=None):
+            tile = sbuf(name, [P, PACK, Q], F32, tag)
             nc.sync.dma_start(tile[:], rows.rearrange("(p j) w -> p j w", j=PACK))
             return tile
 
+        nc.sync.dma_start(age_row[0:32, :], age[0:32, :])
         rate_col = sbuf("rate_col", [P, 1], F32)
         nc.sync.dma_start(rate_col[:], rate)
+        load_scale_rows(nc.sync, key_bytes, keys_scales)
         key_words = load_words("key_words", keys_words)
-        load_scale_rows(nc.scalar, key_bytes, keys_scales)
-        nc.scalar.dma_start(age_row[0:1, :], age[0:1, :])
         query_raw = load_rows("query_raw", query)
-        val_words = load_words("val_words", vals_words)
-        dquery_raw = load_rows("dquery_raw", dquery)
-        load_scale_rows(nc.sync, val_bytes, vals_scales)
-        gout_raw = load_rows("gout_raw", gout)
         size_cols = sbuf("size_cols", [P, SLOT_TILES], F32)
         nc.sync.dma_start(size_cols[:], size.rearrange("o (p c) -> p (o c)", p=P))
+        load_scale_rows(nc.sync, val_bytes, vals_scales)
+        val_words = load_words("val_words", vals_words)
+        gout_raw = load_rows("gout_raw", gout)
+        dquery_raw = load_rows("dquery_raw", dquery)
         reserve_col = sbuf("reserve_col", [P, 1], F32)
         nc.sync.dma_start(reserve_col[:], reserve)
         base_sb = sbuf("base_sb", [P, T], F32)
         nc.sync.dma_start(base_sb[:], base)
 
-        warm = sbuf("warm", [P, 1], F32)
-        nc.scalar.activation(warm[:], ident[:, 0:1], ACT.Exp)
+        warmed = sbuf("warmed", [P, 1], F32)
+        nc.scalar.activation(warmed[:], warm[:], ACT.Exp)
 
         def gather(name, window, dtype, tag=None):
             tile = sbuf(name, [P, I], dtype, tag)
             nc.vector.tensor_copy(tile[:], window.indirect(offsets[:]))
             return tile
 
-        def interleave(name, raw):
-            tile = sbuf(name, [P, Q, PACK], BF16)
+        def interleave(name, raw, tag=None):
+            tile = sbuf(name, [P, Q, PACK], BF16, tag)
             nc.scalar.copy(tile[:], raw[:].rearrange("p j w -> p w j"))
             return tile
 
@@ -104,11 +111,9 @@ def tile_attend_hvfadereserve_s_kernel(tc, query, keys_words, keys_scales, age, 
                                     rhs=rows[0][:].bitcast(FP8X4), rhs_scale=rows[1][:], start=True, stop=True)
             return bank
 
-        key_scale_slots = gather("key_scale_slots", key_bytes[:], U8)
         age_slots = gather("age_slots", age_row[:], F32)
-        placed = sbuf("placed", [P, T], F32, tag="key_bytes")
-        nc.gpsimd.memset(placed[:], 0.0)
-        key_slots = gather("key_slots", key_words[:].bitcast(U32), U32, tag="age_row")
+        key_scale_slots = gather("key_scale_slots", key_bytes[:], U8, tag="age_row")
+        key_slots = gather("key_slots", key_words[:].bitcast(U32), U32, tag="key_bytes")
         query_mx = quantize("query", interleave("query_bf", query_raw), "key_words")
 
         rate_rows = ps.tile([P, Q], F32, name="rate_rows")
@@ -126,6 +131,13 @@ def tile_attend_hvfadereserve_s_kernel(tc, query, keys_words, keys_scales, age, 
             nc.tensor.matmul(x[:, c * P : (c + 1) * P], lhsT=fade_t[:, c, :], rhs=ident[:], is_transpose=True,
                              start=(c == 0), stop=False)
 
+        size_rows = ps.tile([P, SLOT_TILES, P], F32, name="size_rows")
+        for c in range(SLOT_TILES):
+            nc.tensor.transpose(size_rows[:, c, :], size_cols[:, c : c + 1].to_broadcast([P, P]), ident[:])
+        weight_rows = sbuf("weight_rows", [P, I], F32, "query_raw")
+        nc.scalar.activation(weight_rows[:].rearrange("p (n c) -> p n c", c=SLOT_TILES),
+                             size_rows[:].rearrange("p c n -> p n c"), ACT.Copy, scale=-512.0)
+
         a_t = slot_major_product("a_t", key_slots, key_scale_slots, query_mx)
         a_t_sb = sbuf("a_t_sb", [P, SLOT_TILES, Q], F32)
         nc.scalar.copy(a_t_sb[:], a_t[:])
@@ -133,24 +145,17 @@ def tile_attend_hvfadereserve_s_kernel(tc, query, keys_words, keys_scales, age, 
             nc.tensor.matmul(x[:, c * P : (c + 1) * P], lhsT=a_t_sb[:, c, :], rhs=ident[:], is_transpose=True,
                              start=False, stop=(c == SLOT_TILES - 1))
 
-        size_rows = ps.tile([P, SLOT_TILES, P], F32, name="size_rows")
-        for c in range(SLOT_TILES):
-            nc.tensor.transpose(size_rows[:, c, :], size_cols[:, c : c + 1].to_broadcast([P, P]), ident[:])
-        weight_rows = sbuf("weight_rows", [P, I], F32)
-        nc.scalar.activation(weight_rows[:].rearrange("p (n c) -> p n c", c=SLOT_TILES),
-                             size_rows[:].rearrange("p c n -> p n c"), ACT.Copy, scale=-512.0)
-
         val_scale_slots = gather("val_scale_slots", val_bytes[:], U8, tag="query_bf")
         val_slots = gather("val_slots", val_words[:].bitcast(U32), U32, tag="val_bytes")
-        gout_mx = quantize("gout", interleave("gout_bf", gout_raw), "val_words")
-        dquery_mx = quantize("dquery", interleave("dquery_bf", dquery_raw), "gout_bf")
+        gout_mx = quantize("gout", interleave("gout_bf", gout_raw, "query_scales"), "val_words")
+        dquery_bf = interleave("dquery_bf", dquery_raw, "key_words")
 
-        neg_x = sbuf("neg_x", [P, I], F32)
+        neg_x = sbuf("neg_x", [P, I], F32, "query_scales")
         neg_max = sbuf("neg_max", [P, 1], F32)
         nc.vector.tensor_scalar(neg_x[:], x[:], -1.0, 0.0, ALU.mult, ALU.min, accum_out=neg_max[:])
         sink = sbuf("sink", [P, 1], F32)
         nc.scalar.activation(sink[:], neg_max[:], ACT.Exp)
-        p = sbuf("p", [P, I], F32)
+        p = sbuf("p", [P, I], F32, "dquery_raw")
         p_sum = sbuf("p_sum", [P, 1], F32)
         nc.scalar.activation(p[:], neg_x[:], ACT.Exp, bias=neg_max[:], scale=-1.0, accum_out=p_sum[:])
         z = sbuf("z", [P, 1], F32)
@@ -163,9 +168,10 @@ def tile_attend_hvfadereserve_s_kernel(tc, query, keys_words, keys_scales, age, 
             return bank
 
         c0 = row_major_product("c0", gout_mx, val_slots, val_scale_slots)
-        ta = row_major_product("ta", dquery_mx, key_slots, key_scale_slots)
         u = sbuf("u", [P, I], F32)
         nc.vector.tensor_tensor(u[:], c0[:], weight_rows[:], ALU.mult)
+        dquery_mx = quantize("dquery", dquery_bf, "query_raw")
+        ta = row_major_product("ta", dquery_mx, key_slots, key_scale_slots)
 
         up = sbuf("up", [P, I], F32)
         up_sum = sbuf("up_sum", [P, 1], F32)

@@ -19,7 +19,7 @@ ACT = mybir.ActivationFunctionType
 P = 128
 PACK = 4
 SLOT_TILES = I // P
-OUT_CHUNKS = 4
+OUT_WIDTHS = (256, 512, 512, 512, 256)
 
 
 def tile_attend_hvfadereserve_s_kernel(tc, query, keys_words, keys_scales, age, rate, reserve, gout,
@@ -42,15 +42,13 @@ def tile_attend_hvfadereserve_s_kernel(tc, query, keys_words, keys_scales, age, 
         key_zero = key_bytes[:].bitcast(I32)
         nc.vector.memset(key_zero[:, : T // 8], 0)
         nc.gpsimd.memset(key_zero[:, T // 8 :], 0)
-        nc.gpsimd.memset(val_bytes[:].bitcast(I32), 0)
-        nc.gpsimd.memset(warm[:], 0.0)
         nc.vector.memset(age_row[64:128, : T - 1], 0.0)
         nc.vector.memset(age_row[64:128, T - 1 :], 0.0)
         ident = sbuf("ident", [P, P], F32)
         make_identity(nc, ident[:])
+        nc.gpsimd.memset(val_bytes[:].bitcast(I32), 0)
+        nc.gpsimd.memset(warm[:], 0.0)
         nc.gpsimd.memset(age_row[32:64, :], 0.0)
-        placed = sbuf("placed", [P, T], F32)
-        nc.gpsimd.memset(placed[:], 0.0)
 
         def load_scale_rows(queue, tile, scales):
             for quad in range(4):
@@ -68,13 +66,13 @@ def tile_attend_hvfadereserve_s_kernel(tc, query, keys_words, keys_scales, age, 
             return tile
 
         nc.sync.dma_start(age_row[0:32, :], age[0:32, :])
-        rate_col = sbuf("rate_col", [P, 1], F32)
-        nc.sync.dma_start(rate_col[:], rate)
-        load_scale_rows(nc.sync, key_bytes, keys_scales)
-        key_words = load_words("key_words", keys_words)
-        query_raw = load_rows("query_raw", query)
         size_cols = sbuf("size_cols", [P, SLOT_TILES], F32)
         nc.sync.dma_start(size_cols[:], size.rearrange("o (p c) -> p (o c)", p=P))
+        load_scale_rows(nc.sync, key_bytes, keys_scales)
+        key_words = load_words("key_words", keys_words)
+        rate_col = sbuf("rate_col", [P, 1], F32)
+        nc.sync.dma_start(rate_col[:], rate)
+        query_raw = load_rows("query_raw", query)
         load_scale_rows(nc.sync, val_bytes, vals_scales)
         val_words = load_words("val_words", vals_words)
         gout_raw = load_rows("gout_raw", gout)
@@ -111,9 +109,16 @@ def tile_attend_hvfadereserve_s_kernel(tc, query, keys_words, keys_scales, age, 
                                     rhs=rows[0][:].bitcast(FP8X4), rhs_scale=rows[1][:], start=True, stop=True)
             return bank
 
-        age_slots = gather("age_slots", age_row[:], F32)
-        key_scale_slots = gather("key_scale_slots", key_bytes[:], U8, tag="age_row")
-        key_slots = gather("key_slots", key_words[:].bitcast(U32), U32, tag="key_bytes")
+        size_rows = ps.tile([P, SLOT_TILES, P], F32, name="size_rows")
+        for c in range(SLOT_TILES):
+            nc.tensor.transpose(size_rows[:, c, :], size_cols[:, c : c + 1].to_broadcast([P, P]), ident[:])
+        weight_rows = sbuf("weight_rows", [P, I], F32)
+        nc.scalar.activation(weight_rows[:].rearrange("p (n c) -> p n c", c=SLOT_TILES),
+                             size_rows[:].rearrange("p c n -> p n c"), ACT.Copy, scale=-512.0)
+
+        key_scale_slots = gather("key_scale_slots", key_bytes[:], U8)
+        age_slots = gather("age_slots", age_row[:], F32, tag="key_bytes")
+        key_slots = gather("key_slots", key_words[:].bitcast(U32), U32, tag="age_row")
         query_mx = quantize("query", interleave("query_bf", query_raw), "key_words")
 
         rate_rows = ps.tile([P, Q], F32, name="rate_rows")
@@ -131,16 +136,10 @@ def tile_attend_hvfadereserve_s_kernel(tc, query, keys_words, keys_scales, age, 
             nc.tensor.matmul(x[:, c * P : (c + 1) * P], lhsT=fade_t[:, c, :], rhs=ident[:], is_transpose=True,
                              start=(c == 0), stop=False)
 
-        size_rows = ps.tile([P, SLOT_TILES, P], F32, name="size_rows")
-        for c in range(SLOT_TILES):
-            nc.tensor.transpose(size_rows[:, c, :], size_cols[:, c : c + 1].to_broadcast([P, P]), ident[:])
-        weight_rows = sbuf("weight_rows", [P, I], F32, "query_raw")
-        nc.scalar.activation(weight_rows[:].rearrange("p (n c) -> p n c", c=SLOT_TILES),
-                             size_rows[:].rearrange("p c n -> p n c"), ACT.Copy, scale=-512.0)
-
         a_t = slot_major_product("a_t", key_slots, key_scale_slots, query_mx)
         a_t_sb = sbuf("a_t_sb", [P, SLOT_TILES, Q], F32)
-        nc.scalar.copy(a_t_sb[:], a_t[:])
+        for half in range(2):
+            nc.scalar.copy(a_t_sb[:, 2 * half : 2 * half + 2, :], a_t[:, 2 * half : 2 * half + 2, :])
         for c in range(SLOT_TILES):
             nc.tensor.matmul(x[:, c * P : (c + 1) * P], lhsT=a_t_sb[:, c, :], rhs=ident[:], is_transpose=True,
                              start=False, stop=(c == SLOT_TILES - 1))
@@ -170,8 +169,10 @@ def tile_attend_hvfadereserve_s_kernel(tc, query, keys_words, keys_scales, age, 
         c0 = row_major_product("c0", gout_mx, val_slots, val_scale_slots)
         u = sbuf("u", [P, I], F32)
         nc.vector.tensor_tensor(u[:], c0[:], weight_rows[:], ALU.mult)
-        dquery_mx = quantize("dquery", dquery_bf, "query_raw")
+        dquery_mx = quantize("dquery", dquery_bf, "weight_rows")
         ta = row_major_product("ta", dquery_mx, key_slots, key_scale_slots)
+        placed = sbuf("placed", [P, T], F32, "key_words")
+        nc.gpsimd.memset(placed[:], 0.0)
 
         up = sbuf("up", [P, I], F32)
         up_sum = sbuf("up_sum", [P, 1], F32)
@@ -200,9 +201,10 @@ def tile_attend_hvfadereserve_s_kernel(tc, query, keys_words, keys_scales, age, 
         nc.scalar.activation(shift_w[:], w[:], ACT.Copy, scale=shift[:])
         nc.vector.tensor_tensor(placed[:].indirect(offsets[:]), part[:], shift_w[:], ALU.add)
 
-        width = T // OUT_CHUNKS
-        for n in range(OUT_CHUNKS):
-            cols = slice(n * width, (n + 1) * width)
+        first = 0
+        for n, width in enumerate(OUT_WIDTHS):
+            cols = slice(first, first + width)
+            first = first + width
             result = sbuf("result%d" % n, [P, width], F32)
             nc.vector.tensor_tensor(result[:], placed[:, cols], base_sb[:, cols], ALU.add)
             (nc.sync, nc.scalar)[n % 2].dma_start(out[:, cols], result[:])

from contextlib import ExitStack

import concourse.mybir as mybir
from concourse.masks import make_identity

D, E, T, I, Q = 512, 512, 2048, 512, 128
FLOPS = 2 * Q * I * (2 * D + E)

F32 = mybir.dt.float32
BF16 = mybir.dt.bfloat16
I32 = mybir.dt.int32
U32 = mybir.dt.uint32
U16 = mybir.dt.uint16
U8 = mybir.dt.uint8
FP8X4 = mybir.dt.float8_e4m3fn_x4
ALU = mybir.AluOpType
ACT = mybir.ActivationFunctionType

P = 128
PACK = 4
SLOT_TILES = I // P
OUT_WIDTHS = (256, 512, 512, 512, 256)


def tile_attend_hvfadereserve_s_kernel(tc, query, keys_words, keys_scales, age, rate, reserve, gout,
                                        vals_words, vals_scales, size, dquery, base, offs, out):
    nc = tc.nc
    with ExitStack() as ctx:
        sb = ctx.enter_context(tc.tile_pool(name="sb", bufs=1))
        ps = ctx.enter_context(tc.psum_pool(name="ps", bufs=1))

        def sbuf(name, shape, dtype, tag=None):
            return sb.tile(shape, dtype, name=name, tag=tag or name, align_bytes=64)

        offsets = sbuf("offsets", [P, I // 16], U16)
        nc.sync.dma_start(offsets[:], offs)

        key_bytes = sbuf("key_bytes", [P, T], U8)
        val_bytes = sbuf("val_bytes", [P, T], U8)
        age_row = sbuf("age_row", [P, T], F32)
        warm = sbuf("warm", [P, 1], F32)
        key_zero = key_bytes[:].bitcast(I32)
        nc.vector.memset(key_zero[:, : T // 8], 0)
        nc.gpsimd.memset(key_zero[:, T // 8 :], 0)
        nc.vector.memset(age_row[64:128, : T - 1], 0.0)
        nc.vector.memset(age_row[64:128, T - 1 :], 0.0)
        ident = sbuf("ident", [P, P], F32)
        make_identity(nc, ident[:])
        nc.gpsimd.memset(val_bytes[:].bitcast(I32), 0)
        nc.gpsimd.memset(warm[:], 0.0)
        nc.gpsimd.memset(age_row[32:64, :], 0.0)

        def load_scale_rows(queue, tile, scales):
            for quad in range(4):
                queue.dma_start(tile[32 * quad : 32 * quad + 4, :].bitcast(I32),
                                scales[0, 4 * quad : 4 * quad + 4, :].bitcast(I32))

        def load_words(name, words, tag=None):
            tile = sbuf(name, [P, T], I32, tag)
            nc.sync.dma_start(tile[:], words[0].rearrange("p n t -> p (n t)").bitcast(I32))
            return tile

        def load_rows(name, rows, tag=None):
            tile = sbuf(name, [P, PACK, Q], F32, tag)
            nc.sync.dma_start(tile[:], rows.rearrange("(p j) w -> p j w", j=PACK))
            return tile

        nc.sync.dma_start(age_row[0:32, :], age[0:32, :])
        size_cols = sbuf("size_cols", [P, SLOT_TILES], F32)
        nc.sync.dma_start(size_cols[:], size.rearrange("o (p c) -> p (o c)", p=P))
        load_scale_rows(nc.sync, key_bytes, keys_scales)
        key_words = load_words("key_words", keys_words)
        rate_col = sbuf("rate_col", [P, 1], F32)
        nc.sync.dma_start(rate_col[:], rate)
        query_raw = load_rows("query_raw", query)
        load_scale_rows(nc.sync, val_bytes, vals_scales)
        val_words = load_words("val_words", vals_words)
        gout_raw = load_rows("gout_raw", gout)
        dquery_raw = load_rows("dquery_raw", dquery)
        reserve_col = sbuf("reserve_col", [P, 1], F32)
        nc.sync.dma_start(reserve_col[:], reserve)
        base_sb = sbuf("base_sb", [P, T], F32)
        nc.sync.dma_start(base_sb[:], base)

        warmed = sbuf("warmed", [P, 1], F32)
        nc.scalar.activation(warmed[:], warm[:], ACT.Exp)

        def gather(name, window, dtype, tag=None):
            tile = sbuf(name, [P, I], dtype, tag)
            nc.vector.tensor_copy(tile[:], window.indirect(offsets[:]))
            return tile

        def interleave(name, raw, tag=None):
            tile = sbuf(name, [P, Q, PACK], BF16, tag)
            nc.scalar.copy(tile[:], raw[:].rearrange("p j w -> p w j"))
            return tile

        def quantize(name, grouped, tag):
            codes = sbuf(name + "_codes", [P, Q], U32, tag)
            scales = sbuf(name + "_scales", [P, Q], U8)
            nc.vector.quantize_mx(codes[:].bitcast(FP8X4), scales[:], grouped[:].rearrange("p w j -> p (w j)"))
            return codes, scales

        def slot_major_product(name, words, scales, rows):
            bank = ps.tile([P, SLOT_TILES, Q], F32, name=name)
            for c in range(SLOT_TILES):
                cols = slice(c * P, (c + 1) * P)
                nc.tensor.matmul_mx(bank[:, c, :], lhsT=words[:, cols].bitcast(FP8X4), lhsT_scale=scales[:, cols],
                                    rhs=rows[0][:].bitcast(FP8X4), rhs_scale=rows[1][:], start=True, stop=True)
            return bank

        size_rows = ps.tile([P, SLOT_TILES, P], F32, name="size_rows")
        for c in range(SLOT_TILES):
            nc.tensor.transpose(size_rows[:, c, :], size_cols[:, c : c + 1].to_broadcast([P, P]), ident[:])
        weight_rows = sbuf("weight_rows", [P, I], F32)
        nc.scalar.activation(weight_rows[:].rearrange("p (n c) -> p n c", c=SLOT_TILES),
                             size_rows[:].rearrange("p c n -> p n c"), ACT.Copy, scale=-512.0)

        key_scale_slots = gather("key_scale_slots", key_bytes[:], U8)
        age_slots = gather("age_slots", age_row[:], F32, tag="key_bytes")
        key_slots = gather("key_slots", key_words[:].bitcast(U32), U32, tag="age_row")
        query_mx = quantize("query", interleave("query_bf", query_raw), "key_words")

        rate_rows = ps.tile([P, Q], F32, name="rate_rows")
        nc.tensor.transpose(rate_rows[:], rate_col[:].to_broadcast([P, P]), ident[:])
        age_turned = ps.tile([P, SLOT_TILES, P], F32, name="age_turned")
        for c in range(SLOT_TILES):
            nc.tensor.transpose(age_turned[:, c, :], age_slots[:, c * P : (c + 1) * P], ident[:])
        neg_age = sbuf("neg_age", [P, SLOT_TILES], F32)
        nc.scalar.activation(neg_age[:], age_turned[:, :, 0], ACT.Copy, scale=-1.0)
        fade_t = sbuf("fade_t", [P, SLOT_TILES, Q], F32)
        for c in range(SLOT_TILES):
            nc.scalar.activation(fade_t[:, c, :], rate_rows[:], ACT.Copy, scale=neg_age[:, c : c + 1])
        x = ps.tile([P, I], F32, name="x")
        for c in range(SLOT_TILES):
            nc.tensor.matmul(x[:, c * P : (c + 1) * P], lhsT=fade_t[:, c, :], rhs=ident[:], is_transpose=True,
                             start=(c == 0), stop=False)

        a_t = slot_major_product("a_t", key_slots, key_scale_slots, query_mx)
        a_t_sb = sbuf("a_t_sb", [P, SLOT_TILES, Q], F32)
        for half in range(2):
            nc.scalar.copy(a_t_sb[:, 2 * half : 2 * half + 2, :], a_t[:, 2 * half : 2 * half + 2, :])
        for c in range(SLOT_TILES):
            nc.tensor.matmul(x[:, c * P : (c + 1) * P], lhsT=a_t_sb[:, c, :], rhs=ident[:], is_transpose=True,
                             start=False, stop=(c == SLOT_TILES - 1))

        val_scale_slots = gather("val_scale_slots", val_bytes[:], U8, tag="query_bf")
        val_slots = gather("val_slots", val_words[:].bitcast(U32), U32, tag="val_bytes")
        gout_mx = quantize("gout", interleave("gout_bf", gout_raw, "query_scales"), "val_words")
        dquery_bf = interleave("dquery_bf", dquery_raw, "key_words")

        neg_x = sbuf("neg_x", [P, I], F32, "query_scales")
        neg_max = sbuf("neg_max", [P, 1], F32)
        nc.vector.tensor_scalar(neg_x[:], x[:], -1.0, 0.0, ALU.mult, ALU.min, accum_out=neg_max[:])
        sink = sbuf("sink", [P, 1], F32)
        nc.scalar.activation(sink[:], neg_max[:], ACT.Exp)
        p = sbuf("p", [P, I], F32, "dquery_raw")
        p_sum = sbuf("p_sum", [P, 1], F32)
        nc.scalar.activation(p[:], neg_x[:], ACT.Exp, bias=neg_max[:], scale=-1.0, accum_out=p_sum[:])
        z = sbuf("z", [P, 1], F32)
        nc.scalar.activation(z[:], sink[:], ACT.Identity, bias=p_sum[:], scale=reserve_col[:])

        def row_major_product(name, rows, words, scales):
            bank = ps.tile([P, I], F32, name=name)
            nc.tensor.matmul_mx(bank[:], lhsT=rows[0][:].bitcast(FP8X4), lhsT_scale=rows[1][:],
                                rhs=words[:].bitcast(FP8X4), rhs_scale=scales[:], start=True, stop=True)
            return bank

        c0 = row_major_product("c0", gout_mx, val_slots, val_scale_slots)
        u = sbuf("u", [P, I], F32)
        nc.vector.tensor_tensor(u[:], c0[:], weight_rows[:], ALU.mult)
        dquery_mx = quantize("dquery", dquery_bf, "weight_rows")
        ta = row_major_product("ta", dquery_mx, key_slots, key_scale_slots)
        placed = sbuf("placed", [P, T], F32, "key_words")
        nc.gpsimd.memset(placed[:], 0.0)

        up = sbuf("up", [P, I], F32)
        up_sum = sbuf("up_sum", [P, 1], F32)
        nc.vector.scalar_tensor_tensor(up[:], p[:], 1.0, u[:], ALU.mult, ALU.mult, accum_out=up_sum[:])
        inv_z = sbuf("inv_z", [P, 1], F32)
        nc.vector.reciprocal(inv_z[:], z[:])
        tw = sbuf("tw", [P, I], F32)
        mean_ta = sbuf("mean_ta", [P, 1], F32)
        nc.vector.scalar_tensor_tensor(tw[:], p[:], inv_z[:], ta[:], ALU.mult, ALU.mult, accum_out=mean_ta[:])
        mean_u = sbuf("mean_u", [P, 1], F32)
        nc.scalar.activation(mean_u[:], up_sum[:], ACT.Copy, scale=inv_z[:])
        w = sbuf("w", [P, I], F32)
        nc.scalar.activation(w[:], p[:], ACT.Copy, scale=inv_z[:])
        neg_mean_ta = sbuf("neg_mean_ta", [P, 1], F32)
        nc.scalar.activation(neg_mean_ta[:], mean_ta[:], ACT.Copy, scale=-1.0)
        up_factor = sbuf("up_factor", [P, 1], F32)
        nc.scalar.activation(up_factor[:], mean_ta[:], ACT.Copy, scale=inv_z[:])
        cross = sbuf("cross", [P, I], F32)
        cross_sum = sbuf("cross_sum", [P, 1], F32)
        nc.vector.scalar_tensor_tensor(cross[:], u[:], mean_u[:], tw[:], ALU.subtract, ALU.mult, accum_out=cross_sum[:])
        part = sbuf("part", [P, I], F32)
        nc.vector.scalar_tensor_tensor(part[:], up[:], up_factor[:], cross[:], ALU.mult, ALU.subtract)
        shift = sbuf("shift", [P, 1], F32)
        nc.scalar.activation(shift[:], mean_u[:], ACT.Identity, bias=cross_sum[:], scale=neg_mean_ta[:])
        shift_w = sbuf("shift_w", [P, I], F32)
        nc.scalar.activation(shift_w[:], w[:], ACT.Copy, scale=shift[:])
        nc.vector.tensor_tensor(placed[:].indirect(offsets[:]), part[:], shift_w[:], ALU.add)

        first = 0
        for n, width in enumerate(OUT_WIDTHS):
            cols = slice(first, first + width)
            first = first + width
            result = sbuf("result%d" % n, [P, width], F32)
            nc.vector.tensor_tensor(result[:], placed[:, cols], base_sb[:, cols], ALU.add)
            (nc.sync, nc.scalar)[n % 2].dma_start(out[:, cols], result[:])
